import numpy as np
import ml_dtypes


def mxq(x, axis, fmt="e4m3"):
    dtype, down = {"e4m3": (ml_dtypes.float8_e4m3fn, 7), "e5m2": (ml_dtypes.float8_e5m2, 14)}[fmt]
    v = np.moveaxis(np.asarray(x, np.float32).astype(ml_dtypes.bfloat16).astype(np.float64), axis, -1)
    blocks = v.reshape(v.shape[:-1] + (-1, 32))
    amax = np.abs(blocks).max(-1, keepdims=True)
    byte = np.maximum(np.where(amax > 0, np.frexp(amax)[1] - 1 + 127, 0) - down, 1)
    scale = np.exp2(byte - 127.0)
    codes = (blocks / scale).astype(np.float32).astype(dtype).astype(np.float64)
    return np.moveaxis((codes * scale).reshape(v.shape), -1, axis)


WIDE = False


def mx_kscale(k):
    if not WIDE:
        return np.ones(k)
    levels = np.array([10, -10, 5, -5, 0])
    if k % 512:
        return np.exp2(np.random.permutation(np.resize(levels, k // 32))).repeat(32)
    a = np.empty((k // 512, 16))
    for p in range(k // 512):
        a[p, :8] = np.random.permutation(np.resize(levels, 8))
        for g in range(8):
            far = levels[np.abs(levels - a[p, g]) >= 10]
            a[p, g + 8] = far[np.random.randint(len(far))]
    return np.exp2(a.ravel()).repeat(32)


def f64(x):
    return np.asarray(x).astype(np.float64)


def striped(idx):
    return np.tile(idx.reshape(-1, 16).T, (8, 1)).astype(np.uint16)


def unstriped(offs):
    return offs[:16].T.reshape(-1).astype(np.int64)


E2M1 = np.array([0.0, 0.5, 1.0, 1.5, 2.0, 3.0, 4.0, 6.0, -0.0, -0.5, -1.0, -1.5, -2.0, -3.0, -4.0, -6.0])


def pack_weight(w, fmt):
    k, n = w.shape
    w = f64(np.asarray(w, np.float32).astype(ml_dtypes.bfloat16)).reshape(k // 32, 32, n)
    amax = np.abs(w).max(1)
    if fmt == "e4m3":
        byte = np.frexp(amax)[1] - 1 + 127 - 7
    else:
        mant, ex = np.frexp(amax / 6.0)
        byte = np.where(mant > 0.5, ex, ex - 1) + 127
    byte = np.clip(np.where(amax > 0, byte, 1), 1, 254)
    scaled = (w * np.exp2(127.0 - byte)[:, None, :]).reshape(k, n).astype(np.float32)
    by_word = np.ascontiguousarray(scaled.reshape(k // 512, 128, 4, n).transpose(0, 1, 3, 2))
    if fmt == "e4m3":
        words = by_word.astype(ml_dtypes.float8_e4m3fn).view(np.uint8)
    else:
        c = by_word.astype(ml_dtypes.float4_e2m1fn).view(np.uint8) & 0xF
        words = (c[..., 0::2] | (c[..., 1::2] << 4)).reshape(k // 512, 128, 2 * n)
    return np.ascontiguousarray(words), np.ascontiguousarray(byte.astype(np.uint8).reshape(k // 512, 16, n))


def unpack_weight(words, scales, fmt):
    g, _, n = scales.shape
    words = np.ascontiguousarray(words).reshape(g, 128, n, -1)
    if fmt == "e4m3":
        vals = words.view(ml_dtypes.float8_e4m3fn).astype(np.float64)
    else:
        nib = np.empty((g, 128, n, 4), np.uint8)
        nib[..., 0::2] = words & 0xF
        nib[..., 1::2] = words >> 4
        vals = E2M1[nib]
    vals = vals * np.repeat(np.exp2(scales.astype(np.float64) - 127.0), 8, axis=1)[..., None]
    return vals.transpose(0, 1, 3, 2).reshape(g * 512, n)


def gelu(v):
    return 0.5 * v * (1.0 + np.tanh(np.sqrt(2.0 / np.pi) * (v + 0.044715 * v**3)))


K, H, T, S, T3, S2, P = 1536, 512, 2048, 1024, 2048, 512, 512

def setup_inputs():
    n = np.random.standard_normal
    s = mx_kscale(K)[:, None]
    u = mx_kscale(H)[:, None]
    tab_words, tab_scales = pack_weight(n((K, T)) * s, "e4m3")
    tab2_words, tab2_scales = pack_weight(n((H, T3)) / np.sqrt(H) / u, "e4m3")
    w1 = 0.65 * n((K, H)) / np.sqrt(K) / s * u.T
    w2_words, w2_scales = pack_weight(1.2 * n((K, H)) / np.sqrt(K) / s, "e2m1")
    return {
        "tab_words": tab_words, "tab_scales": tab_scales,
        "offs": striped(np.random.permutation(T)[:S]),
        "tab2_words": tab2_words, "tab2_scales": tab2_scales,
        "offs2": striped(np.random.permutation(T3)[:S2]),
        "pos1": striped(np.random.permutation(S)[:P]),
        "pos2": striped(np.random.permutation(S)[:P]),
        "w1": w1.astype(np.float32),
        "w2_words": w2_words, "w2_scales": w2_scales,
        "b2": (0.5 * n(H)).astype(np.float32),
        "lift": (np.random.uniform(0.6, 1.2, H) * u[:, 0]).astype(np.float32),
        "gain": np.random.uniform(3.0, 7.0, S2).astype(np.float32),
    }

def reference(tab_words, tab_scales, offs, tab2_words, tab2_scales, offs2, pos1, pos2,
              w1, w2_words, w2_scales, b2, lift, gain):
    v = unpack_weight(tab_words, tab_scales, "e4m3")[:, unstriped(offs)]
    v2 = unpack_weight(tab2_words, tab2_scales, "e4m3")[:, unstriped(offs2)]
    w2 = unpack_weight(w2_words, w2_scales, "e2m1")
    h = mxq(f64(w1), 0, "e4m3").T @ v
    f = np.tanh((w2.T @ v) + f64(b2)[:, None]) * f64(lift)[:, None]
    e = np.abs(v2.T @ mxq(h, 0, "e4m3")) - (v2.T @ mxq(f, 0, "e4m3"))
    top = e.max(axis=1)
    a = np.exp(e[:, unstriped(pos1)] - top[:, None])
    return f64(gain)[:, None] * a * e[:, unstriped(pos2)]

@@ -1,0 +1,274 @@
+from contextlib import ExitStack
+
+import concourse.mybir as mybir
+
+K, H, T, S, T3, S2, NP = 1536, 512, 2048, 1024, 2048, 512, 512
+FLOPS = 2 * (2 * K * H * S + 2 * H * S2 * S)
+
+F32 = mybir.dt.float32
+BF16 = mybir.dt.bfloat16
+I32 = mybir.dt.int32
+U32 = mybir.dt.uint32
+U16 = mybir.dt.uint16
+U8 = mybir.dt.uint8
+FP8X4 = mybir.dt.float8_e4m3fn_x4
+FP4X4 = mybir.dt.float4_e2m1fn_x4
+ACT = mybir.ActivationFunctionType
+ALU = mybir.AluOpType
+AX = mybir.AxisListType
+
+P = 128
+PACK = 4
+PASSES = K // (P * PACK)
+HALF = 512
+HALVES = S // HALF
+CHUNK = 128
+MT = S2 // P
+ROW0 = 32 - 4 * PASSES
+LIVE = 100
+
+
+def tile_list_pension_affidavits_kernel(
+    tc, tab_words, tab_scales, offs, tab2_words, tab2_scales, offs2, pos1, pos2,
+    w1, w2_words, w2_scales, b2, lift, gain, out,
+):
+    nc = tc.nc
+    with ExitStack() as ctx:
+        sb = ctx.enter_context(tc.tile_pool(name="sb", bufs=1))
+        stage = ctx.enter_context(tc.tile_pool(name="stage", bufs=3))
+        psum = ctx.enter_context(tc.psum_pool(name="psum", bufs=8))
+
+        def tile(name, shape, dtype):
+            return sb.tile(shape, dtype, name=name, align_bytes=64)
+
+        def bank(shape):
+            return psum.tile(shape, F32, name="bank")
+
+        idx = tile("idx", [P, S // 16], U16)
+        idx2 = tile("idx2", [P, S2 // 16], U16)
+        p1 = tile("p1", [P, NP // 16], U16)
+        p2 = tile("p2", [P, NP // 16], U16)
+
+        v_win, w1_raw = {}, {}
+        v_sc_win = tile("v_sc_win", [P, T], U8)
+        v2_sc_win = tile("v2_sc_win", [P, T3], U8)
+        w2_raw = tile("w2_raw", [P, PASSES * H], U16)
+        w2_sc_raw = tile("w2_sc_raw", [P, PASSES * H], U8)
+        b2_sb = tile("b2_sb", [P, PACK], F32)
+        lift_sb = tile("lift_sb", [P, PACK], F32)
+        gain_sb = tile("gain_sb", [P, MT], F32)
+        v_sc = [tile(f"v_sc{a}", [P, S], U8) for a in range(PASSES)]
+
+        v_sc_picked = tile("v_sc_picked", [P, S], U8)
+        for q in range(4):
+            nc.vector.memset(v_sc_win[32 * q : 32 * q + ROW0, :].bitcast(I32), 0)
+
+        def load_table(words):
+            dst = stage.tile([P, T], I32, name="staged", align_bytes=64)
+            nc.sync.dma_start(out=dst[:], in_=words.rearrange("p t i -> p (t i)").bitcast(I32))
+            return dst
+
+        def load_w1(a):
+            w1_raw[a] = stage.tile([P, PACK, H], F32, name="staged", align_bytes=64)
+            nc.sync.dma_start(
+                out=w1_raw[a][:],
+                in_=w1[a * P * PACK : (a + 1) * P * PACK, :].rearrange("(p j) c -> p j c", j=PACK))
+
+        nc.sync.dma_start(idx[:], offs)
+        for q in range(4):
+            (nc.scalar if q < 2 else nc.gpsimd).dma_start(
+                out=v_sc_win[32 * q + ROW0 : 32 * q + 32, :].bitcast(I32),
+                in_=tab_scales[:, 4 * q : 4 * q + 4, :].bitcast(I32))
+        v_win[0] = load_table(tab_words[0])
+        nc.gpsimd.memset(w2_sc_raw[:].bitcast(I32), 0)
+        for a in range(PASSES):
+            nc.gpsimd.memset(v_sc[a][96:, :].bitcast(I32), 0)
+        nc.gpsimd.memset(v2_sc_win[:].bitcast(I32), 0)
+        load_w1(0)
+        v_win[1] = load_table(tab_words[1])
+        nc.sync.dma_start(
+            out=w2_raw[:].bitcast(I32).rearrange("p (a c) -> p a c", a=PASSES),
+            in_=w2_words.bitcast(I32).rearrange("a p c -> p a c"))
+        for q in range(4):
+            nc.gpsimd.dma_start(
+                out=w2_sc_raw[32 * q : 32 * q + 4, :].bitcast(I32).rearrange("r (a c) -> r a c", a=PASSES),
+                in_=w2_scales[:, 4 * q : 4 * q + 4, :].bitcast(I32).rearrange("a r c -> r a c"))
+        nc.gpsimd.dma_start(out=b2_sb[:], in_=b2.rearrange("(p t) -> p t", t=PACK))
+        nc.gpsimd.dma_start(out=lift_sb[:], in_=lift.rearrange("(p t) -> p t", t=PACK))
+        for q in range(4):
+            nc.gpsimd.dma_start(
+                out=v2_sc_win[32 * q : 32 * q + 4, :].bitcast(I32),
+                in_=tab2_scales[0, 4 * q : 4 * q + 4, :].bitcast(I32))
+        v_win[2] = load_table(tab_words[2])
+        load_w1(1)
+        load_w1(2)
+        v2_win = load_table(tab2_words[0])
+        nc.sync.dma_start(idx2[:], offs2)
+        nc.sync.dma_start(p1[:], pos1)
+        nc.sync.dma_start(p2[:], pos2)
+        with nc.allow_non_contiguous_dma(reason="one gain value a partition and tile of soldiers"):
+            nc.gpsimd.dma_start(out=gain_sb[:], in_=gain.rearrange("(i p) -> p i", p=P))
+
+        v = [[tile(f"v{a}_{u}", [P, HALF], U32) for u in range(HALVES)] for a in range(PASSES)]
+
+        def gather_v(a, u):
+            cols = slice(u * HALF // 16, (u + 1) * HALF // 16)
+            nc.vector.tensor_copy(out=v[a][u][:], in_=v_win[a][:].bitcast(U32).indirect(idx[:, cols]))
+
+        w1_bf = [tile(f"w1_bf{a}", [P, H * PACK], BF16) for a in range(PASSES)]
+        w1_q = [tile(f"w1_q{a}", [P, H], U32) for a in range(PASSES)]
+        w1_sc = [tile(f"w1_sc{a}", [P, H], U8) for a in range(PASSES)]
+
+        def round_w1(a, copy):
+            copy(
+                out=w1_bf[a][:].rearrange("p (t m j) -> p m t j", t=PACK, j=PACK),
+                in_=w1_raw[a][:].rearrange("p j (m t) -> p m t j", t=PACK))
+
+        def quantize(codes, scales, values):
+            nc.vector.quantize_mx(out=codes[:].bitcast(FP8X4), scales=scales[:], in_=values[:])
+
+        w2 = tile("w2", [P, PASSES * H], U16)
+        w2_sc = tile("w2_sc", [P, PASSES * H], U8)
+
+        nc.vector.tensor_copy(out=v_sc_picked[:], in_=v_sc_win[:].indirect(idx[:]))
+        gather_v(0, 0)
+        gather_v(0, 1)
+        for a in range(PASSES):
+            first = ROW0 + 4 * a
+            nc.scalar.dma_start(
+                out=v_sc[a][0:LIVE, :].bitcast(I32), in_=v_sc_picked[first : first + LIVE, :].bitcast(I32))
+        round_w1(0, nc.scalar.copy)
+        nc.scalar.copy(
+            out=w2[:].rearrange("p (a t m) -> p a t m", a=PASSES, t=PACK),
+            in_=w2_raw[:].rearrange("p (a m t) -> p a t m", a=PASSES, t=PACK))
+        gather_v(1, 0)
+        nc.vector.tensor_copy(
+            out=w2_sc[:].rearrange("p (a t m) -> p a t m", a=PASSES, t=PACK),
+            in_=w2_sc_raw[:].rearrange("p (a m t) -> p a t m", a=PASSES, t=PACK))
+        gather_v(1, 1)
+        quantize(w1_q[0], w1_sc[0], w1_bf[0])
+        v2 = tile("v2", [P, S2], U32)
+        v2_sc = tile("v2_sc", [P, S2], U8)
+        nc.vector.tensor_copy(out=v2_sc[:], in_=v2_sc_win[:].indirect(idx2[:]))
+        gather_v(2, 0)
+        gather_v(2, 1)
+
+        th = [tile(f"th{u}", [P, PACK, HALF], F32) for u in range(HALVES)]
+        f_bf = [tile(f"f_bf{u}", [P, HALF * PACK], BF16) for u in range(HALVES)]
+        h_bf = [tile(f"h_bf{u}", [P, HALF * PACK], BF16) for u in range(HALVES)]
+        f_q = [tile(f"f_q{u}", [P, HALF], U32) for u in range(HALVES)]
+        f_sc = [tile(f"f_sc{u}", [P, HALF], U8) for u in range(HALVES)]
+        h_q = [tile(f"h_q{u}", [P, HALF], U32) for u in range(HALVES)]
+        h_sc = [tile(f"h_sc{u}", [P, HALF], U8) for u in range(HALVES)]
+
+        def f_pass(banks, a, u):
+            for t in range(PACK):
+                cols = slice(a * H + t * P, a * H + (t + 1) * P)
+                nc.tensor.matmul_mx(
+                    out=banks[t][:], lhsT=w2[:, cols].bitcast(FP4X4), lhsT_scale=w2_sc[:, cols],
+                    rhs=v[a][u][:].bitcast(FP8X4), rhs_scale=v_sc[a][:, u * HALF : (u + 1) * HALF],
+                    start=(a == 0), stop=(a == PASSES - 1))
+
+        def h_pass(banks, a, u, c):
+            for t in range(PACK):
+                cols = slice(t * P, (t + 1) * P)
+                nc.tensor.matmul_mx(
+                    out=banks[c][:, t, :], lhsT=w1_q[a][:, cols].bitcast(FP8X4),
+                    lhsT_scale=w1_sc[a][:, cols],
+                    rhs=v[a][u][:, c * CHUNK : (c + 1) * CHUNK].bitcast(FP8X4),
+                    rhs_scale=v_sc[a][:, u * HALF + c * CHUNK : u * HALF + (c + 1) * CHUNK],
+                    start=(a == 0 and t == 0), stop=(a == PASSES - 1 and t == PACK - 1))
+
+        def f_tanh(banks, u):
+            for t in range(PACK):
+                nc.scalar.activation(
+                    out=th[u][:, t, :], in_=banks[t][:], func=ACT.Tanh, bias=b2_sb[:, t : t + 1])
+
+        def f_lift(u):
+            nc.vector.tensor_tensor(
+                out=f_bf[u][:].rearrange("p (c i t) -> p c t i", i=4, t=PACK),
+                in0=th[u][:].rearrange("p t (c i) -> p c t i", i=4),
+                in1=lift_sb[:].unsqueeze(1).unsqueeze(3).to_broadcast([P, HALF // 4, PACK, 4]),
+                op=ALU.mult)
+
+        def h_round(banks, u):
+            for c in range(HALF // CHUNK):
+                nc.scalar.copy(
+                    out=h_bf[u][:, c * CHUNK * PACK : (c + 1) * CHUNK * PACK].rearrange("p (n t) -> p n t", t=PACK),
+                    in_=banks[c][:].rearrange("p t n -> p n t"))
+
+        e = [tile(f"e{m}", [P, S], F32) for m in range(MT)]
+        part = [tile(f"part{m}", [P, HALVES], F32) for m in range(MT)]
+        size = [[tile(f"size{m}_{u}", [P, HALF], F32) for u in range(HALVES)] for m in range(MT)]
+
+        def scores(m, u):
+            cols = slice(m * P, (m + 1) * P)
+            first, second = bank([P, HALF]), bank([P, HALF])
+            for acc, codes, scales in ((first, h_q[u], h_sc[u]), (second, f_q[u], f_sc[u])):
+                nc.tensor.matmul_mx(
+                    out=acc[:], lhsT=v2[:, cols].bitcast(FP8X4), lhsT_scale=v2_sc[:, cols],
+                    rhs=codes[:].bitcast(FP8X4), rhs_scale=scales[:], start=True, stop=True)
+            nc.scalar.activation(out=size[m][u][:], in_=first[:], func=ACT.Abs)
+            nc.vector.tensor_tensor(
+                out=e[m][:, u * HALF : (u + 1) * HALF], in0=size[m][u][:], in1=second[:], op=ALU.subtract)
+
+        def row_max(m, u):
+            nc.vector.reduce_max(out=part[m][:, u : u + 1], in_=e[m][:, u * HALF : (u + 1) * HALF], axis=AX.X)
+
+        f_banks = [[bank([P, HALF]) for t in range(PACK)] for u in range(HALVES)]
+        for a in range(PASSES):
+            for u in range(HALVES):
+                f_pass(f_banks[u], a, u)
+        round_w1(1, nc.scalar.copy)
+        f_tanh(f_banks[0], 0)
+        f_tanh(f_banks[1], 1)
+        quantize(w1_q[1], w1_sc[1], w1_bf[1])
+        round_w1(2, nc.vector.tensor_copy)
+        f_lift(0)
+        quantize(w1_q[2], w1_sc[2], w1_bf[2])
+        h_banks = [[bank([P, PACK, CHUNK]) for c in range(HALF // CHUNK)] for u in range(HALVES)]
+        for a in range(PASSES):
+            for c in range(HALF // CHUNK):
+                h_pass(h_banks[0], a, 0, c)
+        for c in range(HALF // CHUNK):
+            for a in range(PASSES):
+                h_pass(h_banks[1], a, 1, c)
+        quantize(f_q[0], f_sc[0], f_bf[0])
+        nc.vector.tensor_copy(out=v2[:], in_=v2_win[:].bitcast(U32).indirect(idx2[:]))
+        h_round(h_banks[0], 0)
+        f_lift(1)
+        quantize(h_q[0], h_sc[0], h_bf[0])
+        quantize(f_q[1], f_sc[1], f_bf[1])
+        h_round(h_banks[1], 1)
+        for m in range(MT):
+            scores(m, 0)
+        quantize(h_q[1], h_sc[1], h_bf[1])
+        for m in range(MT):
+            row_max(m, 0)
+
+        neg_top = [tile(f"neg_top{m}", [P, 1], F32) for m in range(MT)]
+        weight = [tile(f"weight{m}", [P, NP], F32) for m in range(MT)]
+        widow = [tile(f"widow{m}", [P, NP], F32) for m in range(MT)]
+        result = [tile(f"result{m}", [P, NP], F32) for m in range(MT)]
+
+        def look(m):
+            row_max(m, 1)
+            nc.vector.tensor_scalar(
+                out=neg_top[m][:], in0=part[m][:, 0:1], scalar1=part[m][:, 1:2], scalar2=-1.0,
+                op0=ALU.max, op1=ALU.mult)
+            nc.scalar.activation(out=weight[m][:], in_=e[m][:].indirect(p1[:]), func=ACT.Exp, bias=neg_top[m][:])
+            nc.vector.tensor_copy(out=widow[m][:], in_=e[m][:].indirect(p2[:]))
+
+        def finish(m):
+            nc.vector.scalar_tensor_tensor(
+                out=result[m][:], in0=weight[m][:], scalar=gain_sb[:, m : m + 1], in1=widow[m][:],
+                op0=ALU.mult, op1=ALU.mult)
+            nc.sync.dma_start(out=out[m * P : (m + 1) * P, :], in_=result[m][:])
+
+        for step in range(MT + 2):
+            if step < MT:
+                scores(step, 1)
+            if 1 <= step <= MT:
+                look(step - 1)
+            if step >= 2:
+                finish(step - 2)

@@ -20,12 +20,19 @@ AX = mybir.AxisListType
 P = 128
 PACK = 4
 PASSES = K // (P * PACK)
+QUADS = 4
+QUAD = P // QUADS
+ROWS = 4
+GROUP = 16
+BANKS = 8
 HALF = 512
 HALVES = S // HALF
-CHUNK = 128
-MT = S2 // P
-ROW0 = 32 - 4 * PASSES
-LIVE = 100
+CHUNK = HALF // PACK
+CHUNKS = HALF // CHUNK
+TILES = S2 // P
+RUN = 4
+ROW0 = QUAD - ROWS * PASSES
+SPAN = (QUADS - 1) * QUAD + ROWS
 
 
 def tile_list_pension_affidavits_kernel(
@@ -35,85 +42,81 @@ def tile_list_pension_affidavits_kernel(
     nc = tc.nc
     with ExitStack() as ctx:
         sb = ctx.enter_context(tc.tile_pool(name="sb", bufs=1))
-        stage = ctx.enter_context(tc.tile_pool(name="stage", bufs=3))
-        psum = ctx.enter_context(tc.psum_pool(name="psum", bufs=8))
+        psum = ctx.enter_context(tc.psum_pool(name="psum", bufs=BANKS))
 
-        def tile(name, shape, dtype):
-            return sb.tile(shape, dtype, name=name, align_bytes=64)
+        def tile(name, shape, dtype, room=None):
+            return sb.tile(shape, dtype, name=name, tag=room or name, align_bytes=64)
 
         def bank(shape):
             return psum.tile(shape, F32, name="bank")
 
-        idx = tile("idx", [P, S // 16], U16)
-        idx2 = tile("idx2", [P, S2 // 16], U16)
-        p1 = tile("p1", [P, NP // 16], U16)
-        p2 = tile("p2", [P, NP // 16], U16)
+        idx = tile("idx", [P, S // GROUP], U16)
+        idx2 = tile("idx2", [P, S2 // GROUP], U16)
+        p1 = tile("p1", [P, NP // GROUP], U16)
+        p2 = tile("p2", [P, NP // GROUP], U16)
 
         v_win, w1_raw = {}, {}
         v_sc_win = tile("v_sc_win", [P, T], U8)
-        v2_sc_win = tile("v2_sc_win", [P, T3], U8)
         w2_raw = tile("w2_raw", [P, PASSES * H], U16)
-        w2_sc_raw = tile("w2_sc_raw", [P, PASSES * H], U8)
+        w2_sc_raw = tile("w2_sc_raw", [P, PASSES * H], U8, "room_scales")
         b2_sb = tile("b2_sb", [P, PACK], F32)
         lift_sb = tile("lift_sb", [P, PACK], F32)
-        gain_sb = tile("gain_sb", [P, MT], F32)
         v_sc = [tile(f"v_sc{a}", [P, S], U8) for a in range(PASSES)]
-
         v_sc_picked = tile("v_sc_picked", [P, S], U8)
-        for q in range(4):
-            nc.vector.memset(v_sc_win[32 * q : 32 * q + ROW0, :].bitcast(I32), 0)
 
-        def load_table(words):
-            dst = stage.tile([P, T], I32, name="staged", align_bytes=64)
+        for q in range(QUADS):
+            nc.vector.memset(v_sc_win[QUAD * q : QUAD * q + ROW0, :].bitcast(I32), 0)
+
+        def load_table(words, room):
+            dst = tile("table_words", [P, T], I32, room)
             nc.sync.dma_start(out=dst[:], in_=words.rearrange("p t i -> p (t i)").bitcast(I32))
             return dst
 
-        def load_w1(a):
-            w1_raw[a] = stage.tile([P, PACK, H], F32, name="staged", align_bytes=64)
+        def load_w1(a, room):
+            w1_raw[a] = tile("w1_raw", [P, PACK, H], F32, room)
             nc.sync.dma_start(
                 out=w1_raw[a][:],
                 in_=w1[a * P * PACK : (a + 1) * P * PACK, :].rearrange("(p j) c -> p j c", j=PACK))
 
         nc.sync.dma_start(idx[:], offs)
-        for q in range(4):
-            (nc.scalar if q < 2 else nc.gpsimd).dma_start(
-                out=v_sc_win[32 * q + ROW0 : 32 * q + 32, :].bitcast(I32),
-                in_=tab_scales[:, 4 * q : 4 * q + 4, :].bitcast(I32))
-        v_win[0] = load_table(tab_words[0])
+        for q in range(QUADS):
+            (nc.scalar if q < QUADS // 2 else nc.sync).dma_start(
+                out=v_sc_win[QUAD * q + ROW0 : QUAD * (q + 1), :].bitcast(I32),
+                in_=tab_scales[:, ROWS * q : ROWS * (q + 1), :].bitcast(I32))
+        v_win[0] = load_table(tab_words[0], "room_v0")
         nc.gpsimd.memset(w2_sc_raw[:].bitcast(I32), 0)
         for a in range(PASSES):
-            nc.gpsimd.memset(v_sc[a][96:, :].bitcast(I32), 0)
-        nc.gpsimd.memset(v2_sc_win[:].bitcast(I32), 0)
-        load_w1(0)
-        v_win[1] = load_table(tab_words[1])
+            nc.vector.memset(v_sc[a][P - QUAD :, :].bitcast(I32), 0)
         nc.sync.dma_start(
             out=w2_raw[:].bitcast(I32).rearrange("p (a c) -> p a c", a=PASSES),
             in_=w2_words.bitcast(I32).rearrange("a p c -> p a c"))
-        for q in range(4):
+        load_w1(0, "room_w1")
+        v_win[1] = load_table(tab_words[1], "room_v1")
+        for q in range(QUADS):
             nc.gpsimd.dma_start(
-                out=w2_sc_raw[32 * q : 32 * q + 4, :].bitcast(I32).rearrange("r (a c) -> r a c", a=PASSES),
-                in_=w2_scales[:, 4 * q : 4 * q + 4, :].bitcast(I32).rearrange("a r c -> r a c"))
-        nc.gpsimd.dma_start(out=b2_sb[:], in_=b2.rearrange("(p t) -> p t", t=PACK))
-        nc.gpsimd.dma_start(out=lift_sb[:], in_=lift.rearrange("(p t) -> p t", t=PACK))
-        for q in range(4):
+                out=w2_sc_raw[QUAD * q : QUAD * q + ROWS, :].bitcast(I32).rearrange("r (a c) -> r a c", a=PASSES),
+                in_=w2_scales[:, ROWS * q : ROWS * (q + 1), :].bitcast(I32).rearrange("a r c -> r a c"))
+        v2_sc_win = tile("v2_sc_win", [P, T3], U8, "room_scales")
+        nc.gpsimd.memset(v2_sc_win[:].bitcast(I32), 0)
+        for q in range(QUADS):
             nc.gpsimd.dma_start(
-                out=v2_sc_win[32 * q : 32 * q + 4, :].bitcast(I32),
-                in_=tab2_scales[0, 4 * q : 4 * q + 4, :].bitcast(I32))
-        v_win[2] = load_table(tab_words[2])
-        load_w1(1)
-        load_w1(2)
-        v2_win = load_table(tab2_words[0])
+                out=v2_sc_win[QUAD * q : QUAD * q + ROWS, :].bitcast(I32),
+                in_=tab2_scales[0, ROWS * q : ROWS * (q + 1), :].bitcast(I32))
+        nc.sync.dma_start(out=b2_sb[:], in_=b2.rearrange("(p t) -> p t", t=PACK))
+        nc.sync.dma_start(out=lift_sb[:], in_=lift.rearrange("(p t) -> p t", t=PACK))
+        v_win[2] = load_table(tab_words[2], "room_v2")
         nc.sync.dma_start(idx2[:], offs2)
         nc.sync.dma_start(p1[:], pos1)
         nc.sync.dma_start(p2[:], pos2)
-        with nc.allow_non_contiguous_dma(reason="one gain value a partition and tile of soldiers"):
-            nc.gpsimd.dma_start(out=gain_sb[:], in_=gain.rearrange("(i p) -> p i", p=P))
+        load_w1(1, "room_v0")
+        load_w1(2, "room_w1")
+        v2_win = load_table(tab2_words[0], "room_v2")
 
         v = [[tile(f"v{a}_{u}", [P, HALF], U32) for u in range(HALVES)] for a in range(PASSES)]
 
         def gather_v(a, u):
-            cols = slice(u * HALF // 16, (u + 1) * HALF // 16)
-            nc.vector.tensor_copy(out=v[a][u][:], in_=v_win[a][:].bitcast(U32).indirect(idx[:, cols]))
+            entries = slice(u * HALF // GROUP, (u + 1) * HALF // GROUP)
+            nc.vector.tensor_copy(out=v[a][u][:], in_=v_win[a][:].bitcast(U32).indirect(idx[:, entries]))
 
         w1_bf = [tile(f"w1_bf{a}", [P, H * PACK], BF16) for a in range(PASSES)]
         w1_q = [tile(f"w1_q{a}", [P, H], U32) for a in range(PASSES)]
@@ -123,6 +126,9 @@ def tile_list_pension_affidavits_kernel(
             copy(
                 out=w1_bf[a][:].rearrange("p (t m j) -> p m t j", t=PACK, j=PACK),
                 in_=w1_raw[a][:].rearrange("p j (m t) -> p m t j", t=PACK))
+
+        def copy_by_activation(out, in_):
+            nc.scalar.activation(out=out, in_=in_, func=ACT.Copy)
 
         def quantize(codes, scales, values):
             nc.vector.quantize_mx(out=codes[:].bitcast(FP8X4), scales=scales[:], in_=values[:])
@@ -134,26 +140,28 @@ def tile_list_pension_affidavits_kernel(
         gather_v(0, 0)
         gather_v(0, 1)
         for a in range(PASSES):
-            first = ROW0 + 4 * a
-            nc.scalar.dma_start(
-                out=v_sc[a][0:LIVE, :].bitcast(I32), in_=v_sc_picked[first : first + LIVE, :].bitcast(I32))
-        round_w1(0, nc.scalar.copy)
+            first = ROW0 + ROWS * a
+            nc.gpsimd.dma_start(
+                out=v_sc[a][0:SPAN, :].bitcast(I32), in_=v_sc_picked[first : first + SPAN, :].bitcast(I32))
         nc.scalar.copy(
             out=w2[:].rearrange("p (a t m) -> p a t m", a=PASSES, t=PACK),
             in_=w2_raw[:].rearrange("p (a m t) -> p a t m", a=PASSES, t=PACK))
-        gather_v(1, 0)
-        nc.vector.tensor_copy(
+        round_w1(0, copy_by_activation)
+        nc.gpsimd.tensor_copy(
             out=w2_sc[:].rearrange("p (a t m) -> p a t m", a=PASSES, t=PACK),
             in_=w2_sc_raw[:].rearrange("p (a m t) -> p a t m", a=PASSES, t=PACK))
+        gather_v(1, 0)
         gather_v(1, 1)
         quantize(w1_q[0], w1_sc[0], w1_bf[0])
+        gain_sb = tile("gain_sb", [P, TILES], F32, "room_v1")
+        with nc.allow_non_contiguous_dma(reason="one gain value a partition and tile of soldiers"):
+            nc.gpsimd.dma_start(out=gain_sb[:], in_=gain.rearrange("(i p) -> p i", p=P))
         v2 = tile("v2", [P, S2], U32)
-        v2_sc = tile("v2_sc", [P, S2], U8)
-        nc.vector.tensor_copy(out=v2_sc[:], in_=v2_sc_win[:].indirect(idx2[:]))
+        v2_sc = tile("v2_sc", [P, S2], U8, "room_w1")
         gather_v(2, 0)
         gather_v(2, 1)
 
-        th = [tile(f"th{u}", [P, PACK, HALF], F32) for u in range(HALVES)]
+        bent = tile("bent", [P, HALVES, PACK, HALF], F32, "room_v0")
         f_bf = [tile(f"f_bf{u}", [P, HALF * PACK], BF16) for u in range(HALVES)]
         h_bf = [tile(f"h_bf{u}", [P, HALF * PACK], BF16) for u in range(HALVES)]
         f_q = [tile(f"f_q{u}", [P, HALF], U32) for u in range(HALVES)]
@@ -182,38 +190,38 @@ def tile_list_pension_affidavits_kernel(
         def f_tanh(banks, u):
             for t in range(PACK):
                 nc.scalar.activation(
-                    out=th[u][:, t, :], in_=banks[t][:], func=ACT.Tanh, bias=b2_sb[:, t : t + 1])
+                    out=bent[:, u, t, :], in_=banks[t][:], func=ACT.Tanh, bias=b2_sb[:, t : t + 1])
 
         def f_lift(u):
             nc.vector.tensor_tensor(
-                out=f_bf[u][:].rearrange("p (c i t) -> p c t i", i=4, t=PACK),
-                in0=th[u][:].rearrange("p t (c i) -> p c t i", i=4),
-                in1=lift_sb[:].unsqueeze(1).unsqueeze(3).to_broadcast([P, HALF // 4, PACK, 4]),
+                out=f_bf[u][:].rearrange("p (c i t) -> p c t i", i=RUN, t=PACK),
+                in0=bent[:, u, :, :].rearrange("p t (c i) -> p c t i", i=RUN),
+                in1=lift_sb[:].unsqueeze(1).unsqueeze(3).to_broadcast([P, HALF // RUN, PACK, RUN]),
                 op=ALU.mult)
 
         def h_round(banks, u):
-            for c in range(HALF // CHUNK):
+            for c in range(CHUNKS):
                 nc.scalar.copy(
                     out=h_bf[u][:, c * CHUNK * PACK : (c + 1) * CHUNK * PACK].rearrange("p (n t) -> p n t", t=PACK),
                     in_=banks[c][:].rearrange("p t n -> p n t"))
 
-        e = [tile(f"e{m}", [P, S], F32) for m in range(MT)]
-        part = [tile(f"part{m}", [P, HALVES], F32) for m in range(MT)]
-        size = [[tile(f"size{m}_{u}", [P, HALF], F32) for u in range(HALVES)] for m in range(MT)]
+        e = [tile(f"e{i}", [P, S], F32) for i in range(TILES)]
+        half_top = [tile(f"half_top{i}", [P, HALVES], F32) for i in range(TILES)]
+        size = [[tile(f"size{i}_{u}", [P, HALF], F32) for u in range(HALVES)] for i in range(TILES)]
 
-        def scores(m, u):
-            cols = slice(m * P, (m + 1) * P)
-            first, second = bank([P, HALF]), bank([P, HALF])
-            for acc, codes, scales in ((first, h_q[u], h_sc[u]), (second, f_q[u], f_sc[u])):
+        def scores(i, u):
+            cols = slice(i * P, (i + 1) * P)
+            with_h, with_f = bank([P, HALF]), bank([P, HALF])
+            for acc, codes, scales in ((with_h, h_q[u], h_sc[u]), (with_f, f_q[u], f_sc[u])):
                 nc.tensor.matmul_mx(
                     out=acc[:], lhsT=v2[:, cols].bitcast(FP8X4), lhsT_scale=v2_sc[:, cols],
                     rhs=codes[:].bitcast(FP8X4), rhs_scale=scales[:], start=True, stop=True)
-            nc.scalar.activation(out=size[m][u][:], in_=first[:], func=ACT.Abs)
+            nc.scalar.activation(out=size[i][u][:], in_=with_h[:], func=ACT.Abs)
             nc.vector.tensor_tensor(
-                out=e[m][:, u * HALF : (u + 1) * HALF], in0=size[m][u][:], in1=second[:], op=ALU.subtract)
+                out=e[i][:, u * HALF : (u + 1) * HALF], in0=size[i][u][:], in1=with_f[:], op=ALU.subtract)
 
-        def row_max(m, u):
-            nc.vector.reduce_max(out=part[m][:, u : u + 1], in_=e[m][:, u * HALF : (u + 1) * HALF], axis=AX.X)
+        def row_max(i, u):
+            nc.vector.reduce_max(out=half_top[i][:, u : u + 1], in_=e[i][:, u * HALF : (u + 1) * HALF], axis=AX.X)
 
         f_banks = [[bank([P, HALF]) for t in range(PACK)] for u in range(HALVES)]
         for a in range(PASSES):
@@ -222,53 +230,53 @@ def tile_list_pension_affidavits_kernel(
         round_w1(1, nc.scalar.copy)
         f_tanh(f_banks[0], 0)
         f_tanh(f_banks[1], 1)
-        quantize(w1_q[1], w1_sc[1], w1_bf[1])
         round_w1(2, nc.vector.tensor_copy)
-        f_lift(0)
+        quantize(w1_q[1], w1_sc[1], w1_bf[1])
         quantize(w1_q[2], w1_sc[2], w1_bf[2])
-        h_banks = [[bank([P, PACK, CHUNK]) for c in range(HALF // CHUNK)] for u in range(HALVES)]
+        h_banks = [[bank([P, PACK, CHUNK]) for c in range(CHUNKS)] for u in range(HALVES)]
         for a in range(PASSES):
-            for c in range(HALF // CHUNK):
+            for c in range(CHUNKS):
                 h_pass(h_banks[0], a, 0, c)
-        for c in range(HALF // CHUNK):
+        for c in range(CHUNKS):
             for a in range(PASSES):
                 h_pass(h_banks[1], a, 1, c)
-        quantize(f_q[0], f_sc[0], f_bf[0])
+        f_lift(0)
+        nc.vector.tensor_copy(out=v2_sc[:], in_=v2_sc_win[:].indirect(idx2[:]))
         nc.vector.tensor_copy(out=v2[:], in_=v2_win[:].bitcast(U32).indirect(idx2[:]))
+        quantize(f_q[0], f_sc[0], f_bf[0])
         h_round(h_banks[0], 0)
-        f_lift(1)
         quantize(h_q[0], h_sc[0], h_bf[0])
-        quantize(f_q[1], f_sc[1], f_bf[1])
+        f_lift(1)
         h_round(h_banks[1], 1)
-        for m in range(MT):
-            scores(m, 0)
         quantize(h_q[1], h_sc[1], h_bf[1])
-        for m in range(MT):
-            row_max(m, 0)
+        quantize(f_q[1], f_sc[1], f_bf[1])
 
-        neg_top = [tile(f"neg_top{m}", [P, 1], F32) for m in range(MT)]
-        weight = [tile(f"weight{m}", [P, NP], F32) for m in range(MT)]
-        widow = [tile(f"widow{m}", [P, NP], F32) for m in range(MT)]
-        result = [tile(f"result{m}", [P, NP], F32) for m in range(MT)]
+        for i in range(TILES):
+            scores(i, 0)
+        for i in range(TILES):
+            row_max(i, 0)
 
-        def look(m):
-            row_max(m, 1)
+        neg_top = [tile(f"neg_top{i}", [P, 1], F32) for i in range(TILES)]
+        weight = [tile(f"weight{i}", [P, NP], F32) for i in range(TILES)]
+        widow = [tile(f"widow{i}", [P, NP], F32) for i in range(TILES)]
+        result = [tile(f"result{i}", [P, NP], F32) for i in range(TILES)]
+
+        def look(i):
+            row_max(i, 1)
             nc.vector.tensor_scalar(
-                out=neg_top[m][:], in0=part[m][:, 0:1], scalar1=part[m][:, 1:2], scalar2=-1.0,
+                out=neg_top[i][:], in0=half_top[i][:, 0:1], scalar1=half_top[i][:, 1:2], scalar2=-1.0,
                 op0=ALU.max, op1=ALU.mult)
-            nc.scalar.activation(out=weight[m][:], in_=e[m][:].indirect(p1[:]), func=ACT.Exp, bias=neg_top[m][:])
-            nc.vector.tensor_copy(out=widow[m][:], in_=e[m][:].indirect(p2[:]))
+            nc.scalar.activation(out=weight[i][:], in_=e[i][:].indirect(p1[:]), func=ACT.Exp, bias=neg_top[i][:])
+            nc.vector.tensor_copy(out=widow[i][:], in_=e[i][:].indirect(p2[:]))
 
-        def finish(m):
+        def finish(i):
             nc.vector.scalar_tensor_tensor(
-                out=result[m][:], in0=weight[m][:], scalar=gain_sb[:, m : m + 1], in1=widow[m][:],
+                out=result[i][:], in0=weight[i][:], scalar=gain_sb[:, i : i + 1], in1=widow[i][:],
                 op0=ALU.mult, op1=ALU.mult)
-            nc.sync.dma_start(out=out[m * P : (m + 1) * P, :], in_=result[m][:])
+            nc.sync.dma_start(out=out[i * P : (i + 1) * P, :], in_=result[i][:])
 
-        for step in range(MT + 2):
-            if step < MT:
-                scores(step, 1)
-            if 1 <= step <= MT:
-                look(step - 1)
-            if step >= 2:
-                finish(step - 2)
+        stages = (lambda i: scores(i, 1), look, finish)
+        for step in range(TILES + len(stages) - 1):
+            for lag, stage in enumerate(stages):
+                if 0 <= step - lag < TILES:
+                    stage(step - lag)

from contextlib import ExitStack

import concourse.mybir as mybir

K, H, T, S, T3, S2, NP = 1536, 512, 2048, 1024, 2048, 512, 512
FLOPS = 2 * (2 * K * H * S + 2 * H * S2 * S)

F32 = mybir.dt.float32
BF16 = mybir.dt.bfloat16
I32 = mybir.dt.int32
U32 = mybir.dt.uint32
U16 = mybir.dt.uint16
U8 = mybir.dt.uint8
FP8X4 = mybir.dt.float8_e4m3fn_x4
FP4X4 = mybir.dt.float4_e2m1fn_x4
ACT = mybir.ActivationFunctionType
ALU = mybir.AluOpType
AX = mybir.AxisListType

P = 128
PACK = 4
PASSES = K // (P * PACK)
QUADS = 4
QUAD = P // QUADS
ROWS = 4
GROUP = 16
BANKS = 8
HALF = 512
HALVES = S // HALF
CHUNK = HALF // PACK
CHUNKS = HALF // CHUNK
TILES = S2 // P
RUN = 4
ROW0 = QUAD - ROWS * PASSES
SPAN = (QUADS - 1) * QUAD + ROWS


def tile_list_pension_affidavits_kernel(
    tc, tab_words, tab_scales, offs, tab2_words, tab2_scales, offs2, pos1, pos2,
    w1, w2_words, w2_scales, b2, lift, gain, out,
):
    nc = tc.nc
    with ExitStack() as ctx:
        sb = ctx.enter_context(tc.tile_pool(name="sb", bufs=1))
        psum = ctx.enter_context(tc.psum_pool(name="psum", bufs=BANKS))

        def tile(name, shape, dtype, room=None):
            return sb.tile(shape, dtype, name=name, tag=room or name, align_bytes=64)

        def bank(shape):
            return psum.tile(shape, F32, name="bank")

        idx = tile("idx", [P, S // GROUP], U16)
        idx2 = tile("idx2", [P, S2 // GROUP], U16)
        p1 = tile("p1", [P, NP // GROUP], U16)
        p2 = tile("p2", [P, NP // GROUP], U16)

        v_win, w1_raw = {}, {}
        v_sc_win = tile("v_sc_win", [P, T], U8)
        w2_raw = tile("w2_raw", [P, PASSES * H], U16)
        w2_sc_raw = tile("w2_sc_raw", [P, PASSES * H], U8, "room_scales")
        b2_sb = tile("b2_sb", [P, PACK], F32)
        lift_sb = tile("lift_sb", [P, PACK], F32)
        v_sc = [tile(f"v_sc{a}", [P, S], U8) for a in range(PASSES)]
        v_sc_picked = tile("v_sc_picked", [P, S], U8)

        for q in range(QUADS):
            nc.vector.memset(v_sc_win[QUAD * q : QUAD * q + ROW0, :].bitcast(I32), 0)

        def load_table(words, room):
            dst = tile("table_words", [P, T], I32, room)
            nc.sync.dma_start(out=dst[:], in_=words.rearrange("p t i -> p (t i)").bitcast(I32))
            return dst

        def load_w1(a, room):
            w1_raw[a] = tile("w1_raw", [P, PACK, H], F32, room)
            nc.sync.dma_start(
                out=w1_raw[a][:],
                in_=w1[a * P * PACK : (a + 1) * P * PACK, :].rearrange("(p j) c -> p j c", j=PACK))

        nc.sync.dma_start(idx[:], offs)
        for q in range(QUADS):
            (nc.scalar if q < QUADS // 2 else nc.sync).dma_start(
                out=v_sc_win[QUAD * q + ROW0 : QUAD * (q + 1), :].bitcast(I32),
                in_=tab_scales[:, ROWS * q : ROWS * (q + 1), :].bitcast(I32))
        v_win[0] = load_table(tab_words[0], "room_v0")
        nc.gpsimd.memset(w2_sc_raw[:].bitcast(I32), 0)
        for a in range(PASSES):
            nc.vector.memset(v_sc[a][P - QUAD :, :].bitcast(I32), 0)
        nc.sync.dma_start(
            out=w2_raw[:].bitcast(I32).rearrange("p (a c) -> p a c", a=PASSES),
            in_=w2_words.bitcast(I32).rearrange("a p c -> p a c"))
        load_w1(0, "room_w1")
        v_win[1] = load_table(tab_words[1], "room_v1")
        for q in range(QUADS):
            nc.gpsimd.dma_start(
                out=w2_sc_raw[QUAD * q : QUAD * q + ROWS, :].bitcast(I32).rearrange("r (a c) -> r a c", a=PASSES),
                in_=w2_scales[:, ROWS * q : ROWS * (q + 1), :].bitcast(I32).rearrange("a r c -> r a c"))
        v2_sc_win = tile("v2_sc_win", [P, T3], U8, "room_scales")
        nc.gpsimd.memset(v2_sc_win[:].bitcast(I32), 0)
        for q in range(QUADS):
            nc.gpsimd.dma_start(
                out=v2_sc_win[QUAD * q : QUAD * q + ROWS, :].bitcast(I32),
                in_=tab2_scales[0, ROWS * q : ROWS * (q + 1), :].bitcast(I32))
        nc.sync.dma_start(out=b2_sb[:], in_=b2.rearrange("(p t) -> p t", t=PACK))
        nc.sync.dma_start(out=lift_sb[:], in_=lift.rearrange("(p t) -> p t", t=PACK))
        v_win[2] = load_table(tab_words[2], "room_v2")
        nc.sync.dma_start(idx2[:], offs2)
        nc.sync.dma_start(p1[:], pos1)
        nc.sync.dma_start(p2[:], pos2)
        load_w1(1, "room_v0")
        load_w1(2, "room_w1")
        v2_win = load_table(tab2_words[0], "room_v2")

        v = [[tile(f"v{a}_{u}", [P, HALF], U32) for u in range(HALVES)] for a in range(PASSES)]

        def gather_v(a, u):
            entries = slice(u * HALF // GROUP, (u + 1) * HALF // GROUP)
            nc.vector.tensor_copy(out=v[a][u][:], in_=v_win[a][:].bitcast(U32).indirect(idx[:, entries]))

        w1_bf = [tile(f"w1_bf{a}", [P, H * PACK], BF16) for a in range(PASSES)]
        w1_q = [tile(f"w1_q{a}", [P, H], U32) for a in range(PASSES)]
        w1_sc = [tile(f"w1_sc{a}", [P, H], U8) for a in range(PASSES)]

        def round_w1(a, copy):
            copy(
                out=w1_bf[a][:].rearrange("p (t m j) -> p m t j", t=PACK, j=PACK),
                in_=w1_raw[a][:].rearrange("p j (m t) -> p m t j", t=PACK))

        def copy_by_activation(out, in_):
            nc.scalar.activation(out=out, in_=in_, func=ACT.Copy)

        def quantize(codes, scales, values):
            nc.vector.quantize_mx(out=codes[:].bitcast(FP8X4), scales=scales[:], in_=values[:])

        w2 = tile("w2", [P, PASSES * H], U16)
        w2_sc = tile("w2_sc", [P, PASSES * H], U8)

        nc.vector.tensor_copy(out=v_sc_picked[:], in_=v_sc_win[:].indirect(idx[:]))
        gather_v(0, 0)
        gather_v(0, 1)
        for a in range(PASSES):
            first = ROW0 + ROWS * a
            nc.gpsimd.dma_start(
                out=v_sc[a][0:SPAN, :].bitcast(I32), in_=v_sc_picked[first : first + SPAN, :].bitcast(I32))
        nc.scalar.copy(
            out=w2[:].rearrange("p (a t m) -> p a t m", a=PASSES, t=PACK),
            in_=w2_raw[:].rearrange("p (a m t) -> p a t m", a=PASSES, t=PACK))
        round_w1(0, copy_by_activation)
        nc.gpsimd.tensor_copy(
            out=w2_sc[:].rearrange("p (a t m) -> p a t m", a=PASSES, t=PACK),
            in_=w2_sc_raw[:].rearrange("p (a m t) -> p a t m", a=PASSES, t=PACK))
        gather_v(1, 0)
        gather_v(1, 1)
        quantize(w1_q[0], w1_sc[0], w1_bf[0])
        gain_sb = tile("gain_sb", [P, TILES], F32, "room_v1")
        with nc.allow_non_contiguous_dma(reason="one gain value a partition and tile of soldiers"):
            nc.gpsimd.dma_start(out=gain_sb[:], in_=gain.rearrange("(i p) -> p i", p=P))
        v2 = tile("v2", [P, S2], U32)
        v2_sc = tile("v2_sc", [P, S2], U8, "room_w1")
        gather_v(2, 0)
        gather_v(2, 1)

        bent = tile("bent", [P, HALVES, PACK, HALF], F32, "room_v0")
        f_bf = [tile(f"f_bf{u}", [P, HALF * PACK], BF16) for u in range(HALVES)]
        h_bf = [tile(f"h_bf{u}", [P, HALF * PACK], BF16) for u in range(HALVES)]
        f_q = [tile(f"f_q{u}", [P, HALF], U32) for u in range(HALVES)]
        f_sc = [tile(f"f_sc{u}", [P, HALF], U8) for u in range(HALVES)]
        h_q = [tile(f"h_q{u}", [P, HALF], U32) for u in range(HALVES)]
        h_sc = [tile(f"h_sc{u}", [P, HALF], U8) for u in range(HALVES)]

        def f_pass(banks, a, u):
            for t in range(PACK):
                cols = slice(a * H + t * P, a * H + (t + 1) * P)
                nc.tensor.matmul_mx(
                    out=banks[t][:], lhsT=w2[:, cols].bitcast(FP4X4), lhsT_scale=w2_sc[:, cols],
                    rhs=v[a][u][:].bitcast(FP8X4), rhs_scale=v_sc[a][:, u * HALF : (u + 1) * HALF],
                    start=(a == 0), stop=(a == PASSES - 1))

        def h_pass(banks, a, u, c):
            for t in range(PACK):
                cols = slice(t * P, (t + 1) * P)
                nc.tensor.matmul_mx(
                    out=banks[c][:, t, :], lhsT=w1_q[a][:, cols].bitcast(FP8X4),
                    lhsT_scale=w1_sc[a][:, cols],
                    rhs=v[a][u][:, c * CHUNK : (c + 1) * CHUNK].bitcast(FP8X4),
                    rhs_scale=v_sc[a][:, u * HALF + c * CHUNK : u * HALF + (c + 1) * CHUNK],
                    start=(a == 0 and t == 0), stop=(a == PASSES - 1 and t == PACK - 1))

        def f_tanh(banks, u):
            for t in range(PACK):
                nc.scalar.activation(
                    out=bent[:, u, t, :], in_=banks[t][:], func=ACT.Tanh, bias=b2_sb[:, t : t + 1])

        def f_lift(u):
            nc.vector.tensor_tensor(
                out=f_bf[u][:].rearrange("p (c i t) -> p c t i", i=RUN, t=PACK),
                in0=bent[:, u, :, :].rearrange("p t (c i) -> p c t i", i=RUN),
                in1=lift_sb[:].unsqueeze(1).unsqueeze(3).to_broadcast([P, HALF // RUN, PACK, RUN]),
                op=ALU.mult)

        def h_round(banks, u):
            for c in range(CHUNKS):
                nc.scalar.copy(
                    out=h_bf[u][:, c * CHUNK * PACK : (c + 1) * CHUNK * PACK].rearrange("p (n t) -> p n t", t=PACK),
                    in_=banks[c][:].rearrange("p t n -> p n t"))

        e = [tile(f"e{i}", [P, S], F32) for i in range(TILES)]
        half_top = [tile(f"half_top{i}", [P, HALVES], F32) for i in range(TILES)]
        size = [[tile(f"size{i}_{u}", [P, HALF], F32) for u in range(HALVES)] for i in range(TILES)]

        def scores(i, u):
            cols = slice(i * P, (i + 1) * P)
            with_h, with_f = bank([P, HALF]), bank([P, HALF])
            for acc, codes, scales in ((with_h, h_q[u], h_sc[u]), (with_f, f_q[u], f_sc[u])):
                nc.tensor.matmul_mx(
                    out=acc[:], lhsT=v2[:, cols].bitcast(FP8X4), lhsT_scale=v2_sc[:, cols],
                    rhs=codes[:].bitcast(FP8X4), rhs_scale=scales[:], start=True, stop=True)
            nc.scalar.activation(out=size[i][u][:], in_=with_h[:], func=ACT.Abs)
            nc.vector.tensor_tensor(
                out=e[i][:, u * HALF : (u + 1) * HALF], in0=size[i][u][:], in1=with_f[:], op=ALU.subtract)

        def row_max(i, u):
            nc.vector.reduce_max(out=half_top[i][:, u : u + 1], in_=e[i][:, u * HALF : (u + 1) * HALF], axis=AX.X)

        f_banks = [[bank([P, HALF]) for t in range(PACK)] for u in range(HALVES)]
        for a in range(PASSES):
            for u in range(HALVES):
                f_pass(f_banks[u], a, u)
        round_w1(1, nc.scalar.copy)
        f_tanh(f_banks[0], 0)
        f_tanh(f_banks[1], 1)
        round_w1(2, nc.vector.tensor_copy)
        quantize(w1_q[1], w1_sc[1], w1_bf[1])
        quantize(w1_q[2], w1_sc[2], w1_bf[2])
        h_banks = [[bank([P, PACK, CHUNK]) for c in range(CHUNKS)] for u in range(HALVES)]
        for a in range(PASSES):
            for c in range(CHUNKS):
                h_pass(h_banks[0], a, 0, c)
        for c in range(CHUNKS):
            for a in range(PASSES):
                h_pass(h_banks[1], a, 1, c)
        f_lift(0)
        nc.vector.tensor_copy(out=v2_sc[:], in_=v2_sc_win[:].indirect(idx2[:]))
        nc.vector.tensor_copy(out=v2[:], in_=v2_win[:].bitcast(U32).indirect(idx2[:]))
        quantize(f_q[0], f_sc[0], f_bf[0])
        h_round(h_banks[0], 0)
        quantize(h_q[0], h_sc[0], h_bf[0])
        f_lift(1)
        h_round(h_banks[1], 1)
        quantize(h_q[1], h_sc[1], h_bf[1])
        quantize(f_q[1], f_sc[1], f_bf[1])

        for i in range(TILES):
            scores(i, 0)
        for i in range(TILES):
            row_max(i, 0)

        neg_top = [tile(f"neg_top{i}", [P, 1], F32) for i in range(TILES)]
        weight = [tile(f"weight{i}", [P, NP], F32) for i in range(TILES)]
        widow = [tile(f"widow{i}", [P, NP], F32) for i in range(TILES)]
        result = [tile(f"result{i}", [P, NP], F32) for i in range(TILES)]

        def look(i):
            row_max(i, 1)
            nc.vector.tensor_scalar(
                out=neg_top[i][:], in0=half_top[i][:, 0:1], scalar1=half_top[i][:, 1:2], scalar2=-1.0,
                op0=ALU.max, op1=ALU.mult)
            nc.scalar.activation(out=weight[i][:], in_=e[i][:].indirect(p1[:]), func=ACT.Exp, bias=neg_top[i][:])
            nc.vector.tensor_copy(out=widow[i][:], in_=e[i][:].indirect(p2[:]))

        def finish(i):
            nc.vector.scalar_tensor_tensor(
                out=result[i][:], in0=weight[i][:], scalar=gain_sb[:, i : i + 1], in1=widow[i][:],
                op0=ALU.mult, op1=ALU.mult)
            nc.sync.dma_start(out=out[i * P : (i + 1) * P, :], in_=result[i][:])

        stages = (lambda i: scores(i, 1), look, finish)
        for step in range(TILES + len(stages) - 1):
            for lag, stage in enumerate(stages):
                if 0 <= step - lag < TILES:
                    stage(step - lag)
